import numpy as np
import ml_dtypes


def mxq(x, axis, fmt="e4m3"):
    dtype, down = {"e4m3": (ml_dtypes.float8_e4m3fn, 7), "e5m2": (ml_dtypes.float8_e5m2, 14)}[fmt]
    v = np.moveaxis(np.asarray(x, np.float32).astype(ml_dtypes.bfloat16).astype(np.float64), axis, -1)
    blocks = v.reshape(v.shape[:-1] + (-1, 32))
    amax = np.abs(blocks).max(-1, keepdims=True)
    byte = np.maximum(np.where(amax > 0, np.frexp(amax)[1] - 1 + 127, 0) - down, 1)
    scale = np.exp2(byte - 127.0)
    codes = (blocks / scale).astype(np.float32).astype(dtype).astype(np.float64)
    return np.moveaxis((codes * scale).reshape(v.shape), -1, axis)


WIDE = False


def mx_kscale(k):
    if not WIDE:
        return np.ones(k)
    levels = np.array([10, -10, 5, -5, 0])
    if k % 512:
        return np.exp2(np.random.permutation(np.resize(levels, k // 32))).repeat(32)
    a = np.empty((k // 512, 16))
    for p in range(k // 512):
        a[p, :8] = np.random.permutation(np.resize(levels, 8))
        for g in range(8):
            far = levels[np.abs(levels - a[p, g]) >= 10]
            a[p, g + 8] = far[np.random.randint(len(far))]
    return np.exp2(a.ravel()).repeat(32)


def f64(x):
    return np.asarray(x).astype(np.float64)


def striped(idx):
    return np.tile(idx.reshape(-1, 16).T, (8, 1)).astype(np.uint16)


def unstriped(offs):
    return offs[:16].T.reshape(-1).astype(np.int64)


E2M1 = np.array([0.0, 0.5, 1.0, 1.5, 2.0, 3.0, 4.0, 6.0, -0.0, -0.5, -1.0, -1.5, -2.0, -3.0, -4.0, -6.0])


def pack_weight(w, fmt):
    k, n = w.shape
    w = f64(np.asarray(w, np.float32).astype(ml_dtypes.bfloat16)).reshape(k // 32, 32, n)
    amax = np.abs(w).max(1)
    if fmt == "e4m3":
        byte = np.frexp(amax)[1] - 1 + 127 - 7
    else:
        mant, ex = np.frexp(amax / 6.0)
        byte = np.where(mant > 0.5, ex, ex - 1) + 127
    byte = np.clip(np.where(amax > 0, byte, 1), 1, 254)
    scaled = (w * np.exp2(127.0 - byte)[:, None, :]).reshape(k, n).astype(np.float32)
    by_word = np.ascontiguousarray(scaled.reshape(k // 512, 128, 4, n).transpose(0, 1, 3, 2))
    if fmt == "e4m3":
        words = by_word.astype(ml_dtypes.float8_e4m3fn).view(np.uint8)
    else:
        c = by_word.astype(ml_dtypes.float4_e2m1fn).view(np.uint8) & 0xF
        words = (c[..., 0::2] | (c[..., 1::2] << 4)).reshape(k // 512, 128, 2 * n)
    return np.ascontiguousarray(words), np.ascontiguousarray(byte.astype(np.uint8).reshape(k // 512, 16, n))


def unpack_weight(words, scales, fmt):
    g, _, n = scales.shape
    words = np.ascontiguousarray(words).reshape(g, 128, n, -1)
    if fmt == "e4m3":
        vals = words.view(ml_dtypes.float8_e4m3fn).astype(np.float64)
    else:
        nib = np.empty((g, 128, n, 4), np.uint8)
        nib[..., 0::2] = words & 0xF
        nib[..., 1::2] = words >> 4
        vals = E2M1[nib]
    vals = vals * np.repeat(np.exp2(scales.astype(np.float64) - 127.0), 8, axis=1)[..., None]
    return vals.transpose(0, 1, 3, 2).reshape(g * 512, n)


def pack_table(v):
    words, scales = pack_weight(v, "e4m3")
    return np.concatenate([words.reshape(words.shape[0], -1), scales.reshape(scales.shape[0], -1)], axis=1)


def unpack_table(tab):
    g, t = tab.shape[0], tab.shape[1] // 528
    return unpack_weight(tab[:, :512 * t].reshape(g, 128, t, 4), tab[:, 512 * t:].reshape(g, 16, t), "e4m3")


def silu(v):
    return v / (1.0 + np.exp(-np.maximum(v, -700.0)))


O, K, M, T, S = 1024, 1536, 1024, 4096, 1536


def setup_inputs():
    n = np.random.standard_normal
    s = mx_kscale(K)[:, None]
    w = n((K, M)) / np.sqrt(K) / s
    p_w4 = pack_weight(w[O:], "e2m1")
    return {
        "tab": pack_table(n((K, T)) * s),
        "w8": (w[:O]).astype(np.float32),
        "w4_words": p_w4[0],
        "w4_scales": p_w4[1],
        "b": (0.3 * n(1024)).astype(np.float32),
        "offs": striped(np.random.permutation(T)[:S]),
    }


def reference(tab, w8, w4_words, w4_scales, b, offs):
    tab_ = unpack_table(tab)[:, unstriped(offs)]
    w8_ = mxq(f64(w8), 0, "e4m3")
    w4_ = unpack_weight(w4_words, w4_scales, "e2m1")
    y = tab_[:O].T @ w8_ + tab_[O:].T @ w4_
    return silu(y + f64(b)[None, :])

@@ -1,0 +1,189 @@
+from contextlib import ExitStack
+
+import concourse.mybir as mybir
+from concourse.masks import make_identity
+
+F32 = mybir.dt.float32
+BF16 = mybir.dt.bfloat16
+I32 = mybir.dt.int32
+U32 = mybir.dt.uint32
+U16 = mybir.dt.uint16
+U8 = mybir.dt.uint8
+FP8X4 = mybir.dt.float8_e4m3fn_x4
+FP4X4 = mybir.dt.float4_e2m1fn_x4
+ADD = mybir.AluOpType.add
+MULT = mybir.AluOpType.mult
+SILU = mybir.ActivationFunctionType.Silu
+
+P = 128
+O, K, M, T, S = 1024, 1536, 1024, 4096, 1536
+FLOPS = 2 * K * M * S
+NH = 512
+PLANE = (4, 8, 0)
+TILES = S // P
+AHEAD = 8
+
+
+def tile_list_tabo_tm_silu_kernel(tc, tab, w8, w4_words, w4_scales, b, offs, out):
+    nc = tc.nc
+    with ExitStack() as ctx:
+        keep = ctx.enter_context(tc.tile_pool(name="keep", bufs=1))
+        zpool = ctx.enter_context(tc.tile_pool(name="zpool", bufs=6))
+        ypool = ctx.enter_context(tc.tile_pool(name="ypool", bufs=8))
+        psum = ctx.enter_context(tc.psum_pool(name="psum", bufs=8))
+
+        offsets = keep.tile([P, S // 16], U16, name="offsets")
+        words = [keep.tile([P, T], I32, name=f"words{a}", align_bytes=64) for a in range(3)]
+        planes = keep.tile([P, T], U8, name="planes", align_bytes=64)
+        gwords = [keep.tile([P, S], U32, name=f"gwords{a}", align_bytes=64) for a in range(3)]
+        gplanes = keep.tile([P, S], U8, name="gplanes", align_bytes=64)
+        raw = {}
+        grouped = {}
+        codes = {}
+        wscale = {}
+        for h in range(2):
+            for a in range(2):
+                raw[h, a] = keep.tile([P, 4, NH], F32, name=f"raw{h}{a}", align_bytes=64)
+                grouped[h, a] = keep.tile([P, NH, 4], BF16, name=f"grouped{h}{a}", align_bytes=64)
+                codes[h, a] = keep.tile([P, NH], U32, name=f"codes{h}{a}", align_bytes=64)
+                wscale[h, a] = keep.tile([P, NH], U8, name=f"wscale{h}{a}", align_bytes=64)
+        w4w = keep.tile([P, 2 * M], U8, name="w4w", align_bytes=64)
+        w4s = keep.tile([P, M], U8, name="w4s", align_bytes=64)
+        brows = keep.tile([P, P], F32, name="brows")
+        bcol = keep.tile([P, P], F32, name="bcol")
+        bias = keep.tile([P, M], F32, name="bias")
+        ident = keep.tile([P, P], F32, name="ident")
+        warm = keep.tile([P, 1], F32, name="warm")
+
+        nc.vector.memset(planes[:].bitcast(I32), 0)
+        nc.vector.memset(brows[:], 0.0)
+        nc.vector.memset(w4s[:].bitcast(I32), 0)
+        for a in (1, 2):
+            nc.vector.memset(words[a][:, 0:8], 0)
+        for h, a in ((0, 1), (1, 0), (1, 1)):
+            nc.vector.memset(raw[h, a][:, 0, 0:8], 0.0)
+        nc.vector.memset(warm[:], 0.0)
+        nc.scalar.activation(warm[:], warm[:], SILU)
+
+        def load_w8(h, a):
+            src = w8[512 * a : 512 * (a + 1), NH * h : NH * (h + 1)]
+            nc.sync.dma_start(out=raw[h, a][:], in_=src.rearrange("(p j) w -> p j w", j=4))
+
+        def load_words(a):
+            src = tab[a, 0 : 512 * T].rearrange("(p x) -> p x", p=P)
+            nc.sync.dma_start(out=words[a][:], in_=src.bitcast(I32))
+
+        nc.sync.dma_start(offsets[:], offs)
+        load_words(0)
+        load_w8(0, 0)
+        for q in range(4):
+            src = tab[0:2, (512 + 4 * q) * T : (516 + 4 * q) * T].rearrange("a (r t) -> a r t", r=4)
+            k = 32 * q + PLANE[0]
+            nc.gpsimd.dma_start(out=planes[k : k + 8, :].bitcast(I32), in_=src.bitcast(I32))
+        for q in range(4):
+            src = tab[2, (512 + 4 * q) * T : (516 + 4 * q) * T].rearrange("(r t) -> r t", r=4)
+            k = 32 * q + PLANE[2]
+            nc.sync.dma_start(out=planes[k : k + 4, :].bitcast(I32), in_=src.bitcast(I32))
+        nc.sync.dma_start(out=brows[0:8, :], in_=b.rearrange("(c p) -> c p", p=P))
+        nc.sync.dma_start(out=w4w[:].bitcast(I32), in_=w4_words[0].bitcast(I32))
+        load_words(1)
+        load_words(2)
+        for q in range(4):
+            nc.sync.dma_start(
+                out=w4s[32 * q : 32 * q + 4, :].bitcast(I32), in_=w4_scales[0, 4 * q : 4 * q + 4, :].bitcast(I32)
+            )
+        load_w8(0, 1)
+        load_w8(1, 0)
+        load_w8(1, 1)
+
+        make_identity(nc, ident[:])
+
+        def interleave(engine, h, a, lo, hi):
+            src = raw[h, a][:, :, lo:hi].rearrange("p j w -> p w j")
+            dst = grouped[h, a][:, lo:hi, :]
+            if engine == "scalar":
+                nc.scalar.copy(dst, src)
+            elif engine == "vector":
+                nc.vector.tensor_copy(dst, src)
+            else:
+                nc.gpsimd.tensor_scalar(dst, src, 1.0, 0.0, MULT, ADD)
+
+        def quantize(h, a):
+            nc.vector.quantize_mx(
+                out=codes[h, a][:].bitcast(FP8X4),
+                scales=wscale[h, a][:],
+                in_=grouped[h, a][:].rearrange("p w j -> p (w j)"),
+            )
+
+        interleave("scalar", 0, 0, 0, NH)
+
+        pt = psum.tile([P, NH], F32, name="acc")
+        nc.tensor.transpose(pt[:, 0:P], brows[:], ident[:])
+        nc.scalar.copy(bcol[:], pt[:, 0:P])
+        for h in range(2):
+            pb = psum.tile([P, NH], F32, name="acc")
+            for c in range(4):
+                col = bcol[:, 4 * h + c : 4 * h + c + 1].to_broadcast([P, P])
+                nc.tensor.transpose(pb[:, c * P : (c + 1) * P], col, ident[:])
+            nc.scalar.copy(bias[:, NH * h : NH * (h + 1)], pb[:])
+
+        def gather_words(a, lo, hi):
+            nc.vector.tensor_copy(
+                gwords[a][:, lo:hi], words[a][:].bitcast(U32).indirect(offsets[:, lo // 16 : hi // 16])
+            )
+
+
+        def mm(acc, t, h, a):
+            cols = slice(t * P, (t + 1) * P)
+            if a < 2:
+                rhs = codes[h, a][:].bitcast(FP8X4)
+                rhs_scale = wscale[h, a][:]
+            else:
+                rhs = w4w[:, 2 * NH * h : 2 * NH * (h + 1)].bitcast(FP4X4)
+                rhs_scale = w4s[:, NH * h : NH * (h + 1)]
+            nc.tensor.matmul_mx(
+                out=acc[:],
+                lhsT=gwords[a][:, cols].bitcast(FP8X4),
+                lhsT_scale=gplanes[PLANE[a] : P, cols],
+                rhs=rhs,
+                rhs_scale=rhs_scale,
+                start=(a == 0),
+                stop=(a == 1),
+            )
+
+        def epilogue(acc, t, h):
+            z = zpool.tile([P, NH], F32, name="z")
+            nc.vector.tensor_tensor(out=z[:], in0=acc[:], in1=bias[:, NH * h : NH * (h + 1)], op=ADD)
+            y = ypool.tile([P, NH], F32, name="y")
+            nc.scalar.activation(y[:], z[:], SILU)
+            nc.sync.dma_start(out=out[t * P : (t + 1) * P, NH * h : NH * (h + 1)], in_=y[:])
+
+        accs = []
+        for t in range(AHEAD):
+            accs.append(psum.tile([P, NH], F32, name="acc"))
+        gather_words(0, 0, S)
+        nc.vector.tensor_copy(gplanes[:], planes[:].indirect(offsets[:]))
+        quantize(0, 0)
+        for t in range(AHEAD):
+            mm(accs[t], t, 0, 0)
+        gather_words(1, 0, S)
+        gather_words(2, 0, AHEAD * P)
+        for t in range(AHEAD):
+            mm(accs[t], t, 0, 2)
+        interleave("scalar", 0, 1, 0, NH // 2)
+        interleave("gpsimd", 0, 1, NH // 2, NH)
+        quantize(0, 1)
+        gather_words(2, AHEAD * P, S)
+        for t in range(AHEAD):
+            mm(accs[t], t, 0, 1)
+            epilogue(accs[t], t, 0)
+        for a in range(2):
+            for lo in (0, NH // 2):
+                interleave("gpsimd", 1, a, lo, lo + NH // 2)
+            quantize(1, a)
+        order = [(t, 0) for t in range(AHEAD, TILES)] + [(t, 1) for t in range(TILES)]
+        for t, h in order:
+            acc = psum.tile([P, NH], F32, name="acc")
+            for a in (0, 2, 1):
+                mm(acc, t, h, a)
+            epilogue(acc, t, h)

@@ -29,7 +29,7 @@ def tile_list_tabo_tm_silu_kernel(tc, tab, w8, w4_words, w4_scales, b, offs, out
     with ExitStack() as ctx:
         keep = ctx.enter_context(tc.tile_pool(name="keep", bufs=1))
         zpool = ctx.enter_context(tc.tile_pool(name="zpool", bufs=6))
-        ypool = ctx.enter_context(tc.tile_pool(name="ypool", bufs=8))
+        ypool = ctx.enter_context(tc.tile_pool(name="ypool", bufs=6))
         psum = ctx.enter_context(tc.psum_pool(name="psum", bufs=8))
 
         offsets = keep.tile([P, S // 16], U16, name="offsets")
@@ -60,6 +60,7 @@ def tile_list_tabo_tm_silu_kernel(tc, tab, w8, w4_words, w4_scales, b, offs, out
         nc.vector.memset(w4s[:].bitcast(I32), 0)
         for a in (1, 2):
             nc.vector.memset(words[a][:, 0:8], 0)
+        nc.vector.memset(w4w[:, 0:32].bitcast(I32), 0)
         for h, a in ((0, 1), (1, 0), (1, 1)):
             nc.vector.memset(raw[h, a][:, 0, 0:8], 0.0)
         nc.vector.memset(warm[:], 0.0)
@@ -84,15 +85,15 @@ def tile_list_tabo_tm_silu_kernel(tc, tab, w8, w4_words, w4_scales, b, offs, out
             src = tab[2, (512 + 4 * q) * T : (516 + 4 * q) * T].rearrange("(r t) -> r t", r=4)
             k = 32 * q + PLANE[2]
             nc.sync.dma_start(out=planes[k : k + 4, :].bitcast(I32), in_=src.bitcast(I32))
+        load_w8(0, 1)
         nc.sync.dma_start(out=brows[0:8, :], in_=b.rearrange("(c p) -> c p", p=P))
-        nc.sync.dma_start(out=w4w[:].bitcast(I32), in_=w4_words[0].bitcast(I32))
         load_words(1)
-        load_words(2)
+        nc.sync.dma_start(out=w4w[:].bitcast(I32), in_=w4_words[0].bitcast(I32))
         for q in range(4):
             nc.sync.dma_start(
                 out=w4s[32 * q : 32 * q + 4, :].bitcast(I32), in_=w4_scales[0, 4 * q : 4 * q + 4, :].bitcast(I32)
             )
-        load_w8(0, 1)
+        load_words(2)
         load_w8(1, 0)
         load_w8(1, 1)
 
@@ -116,6 +117,7 @@ def tile_list_tabo_tm_silu_kernel(tc, tab, w8, w4_words, w4_scales, b, offs, out
             )
 
         interleave("scalar", 0, 0, 0, NH)
+        interleave("scalar", 0, 1, 0, NH)
 
         pt = psum.tile([P, NH], F32, name="acc")
         nc.tensor.transpose(pt[:, 0:P], brows[:], ident[:])
@@ -148,15 +150,24 @@ def tile_list_tabo_tm_silu_kernel(tc, tab, w8, w4_words, w4_scales, b, offs, out
                 rhs=rhs,
                 rhs_scale=rhs_scale,
                 start=(a == 0),
-                stop=(a == 1),
+                stop=(a == 2),
             )
+
+        ybuf = {}
 
         def epilogue(acc, t, h):
             z = zpool.tile([P, NH], F32, name="z")
             nc.vector.tensor_tensor(out=z[:], in0=acc[:], in1=bias[:, NH * h : NH * (h + 1)], op=ADD)
-            y = ypool.tile([P, NH], F32, name="y")
-            nc.scalar.activation(y[:], z[:], SILU)
-            nc.sync.dma_start(out=out[t * P : (t + 1) * P, NH * h : NH * (h + 1)], in_=y[:])
+            paired = (t, h) not in ((0, 0), (1, 0), (TILES - 2, 1), (TILES - 1, 1))
+            n = 2 if paired else 1
+            u = t % 2 if paired else 0
+            if u == 0:
+                ybuf[n] = ypool.tile([P, n, NH], F32, name=f"y{n}")
+            y = ybuf[n]
+            nc.scalar.activation(y[:, u, :], z[:], SILU)
+            if u == n - 1:
+                dst = out[(t - u) * P : (t + 1) * P, NH * h : NH * (h + 1)]
+                nc.sync.dma_start(out=dst.rearrange("(u p) w -> p u w", p=P), in_=y[:])
 
         accs = []
         for t in range(AHEAD):
@@ -164,19 +175,18 @@ def tile_list_tabo_tm_silu_kernel(tc, tab, w8, w4_words, w4_scales, b, offs, out
         gather_words(0, 0, S)
         nc.vector.tensor_copy(gplanes[:], planes[:].indirect(offsets[:]))
         quantize(0, 0)
+        quantize(0, 1)
         for t in range(AHEAD):
             mm(accs[t], t, 0, 0)
         gather_words(1, 0, S)
-        gather_words(2, 0, AHEAD * P)
-        for t in range(AHEAD):
-            mm(accs[t], t, 0, 2)
-        interleave("scalar", 0, 1, 0, NH // 2)
-        interleave("gpsimd", 0, 1, NH // 2, NH)
-        quantize(0, 1)
-        gather_words(2, AHEAD * P, S)
         for t in range(AHEAD):
             mm(accs[t], t, 0, 1)
+        for t in range(AHEAD):
+            if t % 4 == 0:
+                gather_words(2, t * P, t * P + 512)
+            mm(accs[t], t, 0, 2)
             epilogue(accs[t], t, 0)
+        gather_words(2, AHEAD * P, S)
         for a in range(2):
             for lo in (0, NH // 2):
                 interleave("gpsimd", 1, a, lo, lo + NH // 2)
@@ -184,6 +194,6 @@ def tile_list_tabo_tm_silu_kernel(tc, tab, w8, w4_words, w4_scales, b, offs, out
         order = [(t, 0) for t in range(AHEAD, TILES)] + [(t, 1) for t in range(TILES)]
         for t, h in order:
             acc = psum.tile([P, NH], F32, name="acc")
-            for a in (0, 2, 1):
+            for a in range(3):
                 mm(acc, t, h, a)
             epilogue(acc, t, h)

from contextlib import ExitStack

import concourse.mybir as mybir
from concourse.masks import make_identity

F32 = mybir.dt.float32
BF16 = mybir.dt.bfloat16
I32 = mybir.dt.int32
U32 = mybir.dt.uint32
U16 = mybir.dt.uint16
U8 = mybir.dt.uint8
FP8X4 = mybir.dt.float8_e4m3fn_x4
FP4X4 = mybir.dt.float4_e2m1fn_x4
ADD = mybir.AluOpType.add
MULT = mybir.AluOpType.mult
SILU = mybir.ActivationFunctionType.Silu

P = 128
O, K, M, T, S = 1024, 1536, 1024, 4096, 1536
FLOPS = 2 * K * M * S
NH = 512
PLANE = (4, 8, 0)
TILES = S // P
AHEAD = 8


def tile_list_tabo_tm_silu_kernel(tc, tab, w8, w4_words, w4_scales, b, offs, out):
    nc = tc.nc
    with ExitStack() as ctx:
        keep = ctx.enter_context(tc.tile_pool(name="keep", bufs=1))
        zpool = ctx.enter_context(tc.tile_pool(name="zpool", bufs=6))
        ypool = ctx.enter_context(tc.tile_pool(name="ypool", bufs=6))
        psum = ctx.enter_context(tc.psum_pool(name="psum", bufs=8))

        offsets = keep.tile([P, S // 16], U16, name="offsets")
        words = [keep.tile([P, T], I32, name=f"words{a}", align_bytes=64) for a in range(3)]
        planes = keep.tile([P, T], U8, name="planes", align_bytes=64)
        gwords = [keep.tile([P, S], U32, name=f"gwords{a}", align_bytes=64) for a in range(3)]
        gplanes = keep.tile([P, S], U8, name="gplanes", align_bytes=64)
        raw = {}
        grouped = {}
        codes = {}
        wscale = {}
        for h in range(2):
            for a in range(2):
                raw[h, a] = keep.tile([P, 4, NH], F32, name=f"raw{h}{a}", align_bytes=64)
                grouped[h, a] = keep.tile([P, NH, 4], BF16, name=f"grouped{h}{a}", align_bytes=64)
                codes[h, a] = keep.tile([P, NH], U32, name=f"codes{h}{a}", align_bytes=64)
                wscale[h, a] = keep.tile([P, NH], U8, name=f"wscale{h}{a}", align_bytes=64)
        w4w = keep.tile([P, 2 * M], U8, name="w4w", align_bytes=64)
        w4s = keep.tile([P, M], U8, name="w4s", align_bytes=64)
        brows = keep.tile([P, P], F32, name="brows")
        bcol = keep.tile([P, P], F32, name="bcol")
        bias = keep.tile([P, M], F32, name="bias")
        ident = keep.tile([P, P], F32, name="ident")
        warm = keep.tile([P, 1], F32, name="warm")

        nc.vector.memset(planes[:].bitcast(I32), 0)
        nc.vector.memset(brows[:], 0.0)
        nc.vector.memset(w4s[:].bitcast(I32), 0)
        for a in (1, 2):
            nc.vector.memset(words[a][:, 0:8], 0)
        nc.vector.memset(w4w[:, 0:32].bitcast(I32), 0)
        for h, a in ((0, 1), (1, 0), (1, 1)):
            nc.vector.memset(raw[h, a][:, 0, 0:8], 0.0)
        nc.vector.memset(warm[:], 0.0)
        nc.scalar.activation(warm[:], warm[:], SILU)

        def load_w8(h, a):
            src = w8[512 * a : 512 * (a + 1), NH * h : NH * (h + 1)]
            nc.sync.dma_start(out=raw[h, a][:], in_=src.rearrange("(p j) w -> p j w", j=4))

        def load_words(a):
            src = tab[a, 0 : 512 * T].rearrange("(p x) -> p x", p=P)
            nc.sync.dma_start(out=words[a][:], in_=src.bitcast(I32))

        nc.sync.dma_start(offsets[:], offs)
        load_words(0)
        load_w8(0, 0)
        for q in range(4):
            src = tab[0:2, (512 + 4 * q) * T : (516 + 4 * q) * T].rearrange("a (r t) -> a r t", r=4)
            k = 32 * q + PLANE[0]
            nc.gpsimd.dma_start(out=planes[k : k + 8, :].bitcast(I32), in_=src.bitcast(I32))
        for q in range(4):
            src = tab[2, (512 + 4 * q) * T : (516 + 4 * q) * T].rearrange("(r t) -> r t", r=4)
            k = 32 * q + PLANE[2]
            nc.sync.dma_start(out=planes[k : k + 4, :].bitcast(I32), in_=src.bitcast(I32))
        load_w8(0, 1)
        nc.sync.dma_start(out=brows[0:8, :], in_=b.rearrange("(c p) -> c p", p=P))
        load_words(1)
        nc.sync.dma_start(out=w4w[:].bitcast(I32), in_=w4_words[0].bitcast(I32))
        for q in range(4):
            nc.sync.dma_start(
                out=w4s[32 * q : 32 * q + 4, :].bitcast(I32), in_=w4_scales[0, 4 * q : 4 * q + 4, :].bitcast(I32)
            )
        load_words(2)
        load_w8(1, 0)
        load_w8(1, 1)

        make_identity(nc, ident[:])

        def interleave(engine, h, a, lo, hi):
            src = raw[h, a][:, :, lo:hi].rearrange("p j w -> p w j")
            dst = grouped[h, a][:, lo:hi, :]
            if engine == "scalar":
                nc.scalar.copy(dst, src)
            elif engine == "vector":
                nc.vector.tensor_copy(dst, src)
            else:
                nc.gpsimd.tensor_scalar(dst, src, 1.0, 0.0, MULT, ADD)

        def quantize(h, a):
            nc.vector.quantize_mx(
                out=codes[h, a][:].bitcast(FP8X4),
                scales=wscale[h, a][:],
                in_=grouped[h, a][:].rearrange("p w j -> p (w j)"),
            )

        interleave("scalar", 0, 0, 0, NH)
        interleave("scalar", 0, 1, 0, NH)

        pt = psum.tile([P, NH], F32, name="acc")
        nc.tensor.transpose(pt[:, 0:P], brows[:], ident[:])
        nc.scalar.copy(bcol[:], pt[:, 0:P])
        for h in range(2):
            pb = psum.tile([P, NH], F32, name="acc")
            for c in range(4):
                col = bcol[:, 4 * h + c : 4 * h + c + 1].to_broadcast([P, P])
                nc.tensor.transpose(pb[:, c * P : (c + 1) * P], col, ident[:])
            nc.scalar.copy(bias[:, NH * h : NH * (h + 1)], pb[:])

        def gather_words(a, lo, hi):
            nc.vector.tensor_copy(
                gwords[a][:, lo:hi], words[a][:].bitcast(U32).indirect(offsets[:, lo // 16 : hi // 16])
            )


        def mm(acc, t, h, a):
            cols = slice(t * P, (t + 1) * P)
            if a < 2:
                rhs = codes[h, a][:].bitcast(FP8X4)
                rhs_scale = wscale[h, a][:]
            else:
                rhs = w4w[:, 2 * NH * h : 2 * NH * (h + 1)].bitcast(FP4X4)
                rhs_scale = w4s[:, NH * h : NH * (h + 1)]
            nc.tensor.matmul_mx(
                out=acc[:],
                lhsT=gwords[a][:, cols].bitcast(FP8X4),
                lhsT_scale=gplanes[PLANE[a] : P, cols],
                rhs=rhs,
                rhs_scale=rhs_scale,
                start=(a == 0),
                stop=(a == 2),
            )

        ybuf = {}

        def epilogue(acc, t, h):
            z = zpool.tile([P, NH], F32, name="z")
            nc.vector.tensor_tensor(out=z[:], in0=acc[:], in1=bias[:, NH * h : NH * (h + 1)], op=ADD)
            paired = (t, h) not in ((0, 0), (1, 0), (TILES - 2, 1), (TILES - 1, 1))
            n = 2 if paired else 1
            u = t % 2 if paired else 0
            if u == 0:
                ybuf[n] = ypool.tile([P, n, NH], F32, name=f"y{n}")
            y = ybuf[n]
            nc.scalar.activation(y[:, u, :], z[:], SILU)
            if u == n - 1:
                dst = out[(t - u) * P : (t + 1) * P, NH * h : NH * (h + 1)]
                nc.sync.dma_start(out=dst.rearrange("(u p) w -> p u w", p=P), in_=y[:])

        accs = []
        for t in range(AHEAD):
            accs.append(psum.tile([P, NH], F32, name="acc"))
        gather_words(0, 0, S)
        nc.vector.tensor_copy(gplanes[:], planes[:].indirect(offsets[:]))
        quantize(0, 0)
        quantize(0, 1)
        for t in range(AHEAD):
            mm(accs[t], t, 0, 0)
        gather_words(1, 0, S)
        for t in range(AHEAD):
            mm(accs[t], t, 0, 1)
        for t in range(AHEAD):
            if t % 4 == 0:
                gather_words(2, t * P, t * P + 512)
            mm(accs[t], t, 0, 2)
            epilogue(accs[t], t, 0)
        gather_words(2, AHEAD * P, S)
        for a in range(2):
            for lo in (0, NH // 2):
                interleave("gpsimd", 1, a, lo, lo + NH // 2)
            quantize(1, a)
        order = [(t, 0) for t in range(AHEAD, TILES)] + [(t, 1) for t in range(TILES)]
        for t, h in order:
            acc = psum.tile([P, NH], F32, name="acc")
            for a in range(3):
                mm(acc, t, h, a)
            epilogue(acc, t, h)
